import numpy as np, ml_dtypes
CORES = [64,65,66,67,68,69,70,71,72,73,74,75,76,77,78,79,80,81,82,83,84,85,86,87,88,89,90,91,92,93,94,95]
N = 32
PERM = [[0,16],[1,17],[2,18],[3,19],[4,20],[5,21],[6,22],[7,23],[8,24],[9,25],[10,26],[11,27],[12,28],[13,29],[14,30],[15,31],[16,0],[17,1],[18,2],[19,3],[20,4],[21,5],[22,6],[23,7],[24,8],[25,9],[26,10],[27,11],[28,12],[29,13],[30,14],[31,15]]
def setup_inputs(rng):
    return {"x": rng.standard_normal((N, 128, 256), dtype=np.float32).astype(ml_dtypes.bfloat16)}
def reference(x):
    y = np.empty_like(x)
    for s, d in PERM:
        y[d] = x[s]
    return {"y": y}

SCRATCH = {
    "send": ("dram", [128, 256], "bfloat16"),
    "land": ("dram", [128, 256], "bfloat16"),
}
SEMAPHORES = ["loaded", "left", "arrived", "stored"]


def rank_program(g, core, T, topo):
    rank = T.rank_of(core)
    if rank is None:
        return
    perm = T.tables["PERM"]
    dst = [d for s, d in perm if s == rank]
    src = [s for s, d in perm if d == rank]

    if src and src[0] == rank:
        g.sync.dma_start(T.y[:], T.x[:]).then_inc(T.sem.stored, 16)
        g.sync.wait_ge(T.sem.stored, 16)
        return

    if dst:
        g.sync.dma_start(T.send[:], T.x[:]).then_inc(T.sem.loaded, 16)
        g.wait_ge(T.sem.loaded, 16)
        dcore = T.cores[dst[0]]
        rid, pid, _se = topo.addr(dcore)
        g.remote_dma(T.land[:], T.send[:], T.sem.arrived, T.sem.left, pid, rid, topo.mask(core, dcore))

    if src:
        n_eng = bin(topo.mask(T.cores[src[0]], core)).count("1")
        g.scalar.wait_ge(T.sem.arrived, n_eng)
        g.scalar.dma_start(T.y[:], T.land[:]).then_inc(T.sem.stored, 16)
        g.scalar.wait_ge(T.sem.stored, 16)

    if dst:
        g.wait_ge(T.sem.left, bin(topo.mask(core, T.cores[dst[0]])).count("1"))
